import numpy as np
import ml_dtypes


def mxq(x, axis, fmt="e4m3"):
    dtype, down = {"e4m3": (ml_dtypes.float8_e4m3fn, 7), "e5m2": (ml_dtypes.float8_e5m2, 14)}[fmt]
    v = np.moveaxis(np.asarray(x, np.float32).astype(ml_dtypes.bfloat16).astype(np.float64), axis, -1)
    blocks = v.reshape(v.shape[:-1] + (-1, 32))
    amax = np.abs(blocks).max(-1, keepdims=True)
    byte = np.maximum(np.where(amax > 0, np.frexp(amax)[1] - 1 + 127, 0) - down, 1)
    scale = np.exp2(byte - 127.0)
    codes = (blocks / scale).astype(np.float32).astype(dtype).astype(np.float64)
    return np.moveaxis((codes * scale).reshape(v.shape), -1, axis)


WIDE = False


def mx_kscale(k):
    if not WIDE:
        return np.ones(k)
    levels = np.array([10, -10, 5, -5, 0])
    if k % 512:
        return np.exp2(np.random.permutation(np.resize(levels, k // 32))).repeat(32)
    a = np.empty((k // 512, 16))
    for p in range(k // 512):
        a[p, :8] = np.random.permutation(np.resize(levels, 8))
        for g in range(8):
            far = levels[np.abs(levels - a[p, g]) >= 10]
            a[p, g + 8] = far[np.random.randint(len(far))]
    return np.exp2(a.ravel()).repeat(32)


def f64(x):
    return np.asarray(x).astype(np.float64)


def striped(idx):
    return np.tile(idx.reshape(-1, 16).T, (8, 1)).astype(np.uint16)


def unstriped(offs):
    return offs[:16].T.reshape(-1).astype(np.int64)


def striped8(idx):
    return np.concatenate([x.reshape(-1, 16).T for x in idx]).astype(np.uint16)


def runs(offs, k):
    lists = np.stack([offs[16 * r : 16 * r + 16].T.reshape(-1) for r in range(8)]).astype(np.int64)
    return lists[np.arange(k) % 512 // 64]


def pack_weight(w):
    k, n = w.shape
    w = f64(np.asarray(w, np.float32).astype(ml_dtypes.bfloat16)).reshape(k // 32, 32, n)
    amax = np.abs(w).max(1)
    byte = np.clip(np.where(amax > 0, np.frexp(amax)[1] - 1 + 127 - 7, 1), 1, 254)
    scaled = (w * np.exp2(127.0 - byte)[:, None, :]).reshape(k, n).astype(np.float32)
    words = np.ascontiguousarray(scaled.reshape(k // 512, 128, 4, n).transpose(0, 1, 3, 2)).astype(ml_dtypes.float8_e4m3fn).view(np.uint8)
    return words, np.ascontiguousarray(byte.astype(np.uint8).reshape(k // 512, 16, n))


def unpack_weight(words, scales):
    g, p, n, _ = words.shape
    vals = np.ascontiguousarray(words).view(ml_dtypes.float8_e4m3fn).astype(np.float64) * np.repeat(np.exp2(scales.astype(np.float64) - 127.0), 8, axis=1)[..., None]
    return vals.transpose(0, 1, 3, 2).reshape(g * 512, n)


K, T, S, V, H, W = 512, 2048, 512, 512, 512, 256


def setup_inputs():
    n = np.random.standard_normal
    s = mx_kscale(K)[:, None]
    u = mx_kscale(S)
    packed_xT = pack_weight(n((K, T)) * s)
    perm = np.stack([np.random.permutation(V) for _ in range(8)])
    return {
        "x_words": packed_xT[0],
        "x_scales": packed_xT[1],
        "w1": (n((K, H)) / np.sqrt(K) / s).astype(np.float32),
        "w2": (n((K, H)) / np.sqrt(K) / s).astype(np.float32),
        "ga": (np.random.uniform(0.5, 1.5, (H, 1)) * u[:, None]).astype(np.float32),
        "gb": (np.random.uniform(0.5, 1.5, (H, 1)) / u[:, None]).astype(np.float32),
        "offs": striped(np.random.permutation(T)[:S]),
        "two": striped(np.random.permutation(T)[:V]),
        "n1": striped8(np.stack([np.random.permutation(S) for _ in range(8)])),
        "la": striped8(perm[:, :W]),
        "lb": striped8(perm[:, W:]),
    }


def reference(x_words, x_scales, w1, w2, ga, gb, offs, two, n1, la, lb):
    xq = unpack_weight(x_words, x_scales)[:, unstriped(offs)]
    a = mxq(f64(w1), 0, "e4m3").T @ xq
    z = f64(ga) * (np.maximum(a, a[np.arange(H)[:, None], runs(n1, H)]))
    x_two = unpack_weight(x_words, x_scales)[:, unstriped(two)]
    b = mxq(f64(w2), 0, "e4m3").T @ x_two
    z2 = f64(gb) * b
    s = 0.0625 * ((mxq(z, 0, "e4m3").T @ mxq(z2, 0, "e4m3")))
    p = s[np.arange(S)[:, None], runs(la, S)]
    qv = s[np.arange(S)[:, None], runs(lb, S)]
    hb = np.maximum(p, qv)
    ha = p - (0.5 * qv)
    d1 = np.zeros((S, V))
    d1[np.arange(S)[:, None], runs(la, S)] = ha
    out = d1.copy()
    out[np.arange(S)[:, None], runs(lb, S)] = hb
    return out

@@ -1,0 +1,220 @@
+from contextlib import ExitStack
+
+import concourse.mybir as mybir
+
+K, T, S, V, H, W = 512, 2048, 512, 512, 512, 256
+FLOPS = 2 * K * H * S + 2 * K * H * V + 2 * H * S * V
+
+F32 = mybir.dt.float32
+BF16 = mybir.dt.bfloat16
+I32 = mybir.dt.int32
+U32 = mybir.dt.uint32
+U16 = mybir.dt.uint16
+U8 = mybir.dt.uint8
+FP8X4 = mybir.dt.float8_e4m3fn_x4
+ALU = mybir.AluOpType
+ACT = mybir.ActivationFunctionType
+
+P = 128
+PACK = 4
+HALF = 256
+
+
+def tile_picked_keyduel_none_p_kernel(tc, x_words, x_scales, w1, w2, ga, gb, offs, two, n1, la, lb, out):
+    nc = tc.nc
+    with ExitStack() as ctx:
+        lists = ctx.enter_context(tc.tile_pool(name="lists", bufs=1))
+        keep = ctx.enter_context(tc.tile_pool(name="keep", bufs=1))
+        psum = ctx.enter_context(tc.psum_pool(name="psum", bufs=1))
+
+        offs_t = lists.tile([P, S // 16], U16, name="offs_t")
+        two_t = lists.tile([P, V // 16], U16, name="two_t")
+        n1_t = lists.tile([P, S // 16], U16, name="n1_t")
+        la_t = lists.tile([P, W // 16], U16, name="la_t")
+        lb_t = lists.tile([P, W // 16], U16, name="lb_t")
+
+        x_scale_table = keep.tile([P, T], U8, name="x_scale_table", align_bytes=64)
+        x_word_table = keep.tile([P, T], I32, name="x_word_table", align_bytes=64)
+        nc.vector.memset(x_scale_table[:].bitcast(I32), 0)
+        for q in range(4):
+            nc.scalar.dma_start(
+                out=x_scale_table[32 * q : 32 * q + 4, :].bitcast(I32),
+                in_=x_scales[0, 4 * q : 4 * q + 4, :].bitcast(I32),
+            )
+
+        def load_weight_half(w, name, h):
+            raw = keep.tile([P, PACK, HALF], F32, name="%s_raw%d" % (name, h), tag="stage%d" % h)
+            nc.sync.dma_start(out=raw[:], in_=w.rearrange("(p j) c -> p j c", j=PACK)[:, :, h * HALF : (h + 1) * HALF])
+            return raw
+
+        nc.sync.dma_start(offs_t[:], offs)
+        nc.sync.dma_start(two_t[:], two)
+        w1_raw = [load_weight_half(w1, "w1", h) for h in range(2)]
+        ga_t = keep.tile([P, PACK], F32, name="ga_t")
+        gb_t = keep.tile([P, PACK], F32, name="gb_t")
+        nc.sync.dma_start(out=ga_t[:], in_=ga.rearrange("(p t) o -> p (t o)", t=PACK))
+        nc.sync.dma_start(out=x_word_table[:], in_=x_words[0].rearrange("p n r -> p (n r)").bitcast(I32))
+        nc.sync.dma_start(n1_t[:], n1)
+        nc.sync.dma_start(out=gb_t[:], in_=gb.rearrange("(p t) o -> p (t o)", t=PACK))
+        nc.sync.dma_start(la_t[:], la)
+        nc.sync.dma_start(lb_t[:], lb)
+
+        ga_abs = keep.tile([P, PACK], F32, name="ga_abs")
+        nc.scalar.activation(out=ga_abs[:], in_=ga_t[:], func=ACT.Abs)
+
+        def gather_scales(list_t, name):
+            picked = keep.tile([P, S], U8, name=name, align_bytes=64)
+            nc.vector.tensor_copy(picked[:], x_scale_table[:].indirect(list_t[:]))
+            return picked
+
+        def gather_words(list_t, name):
+            picked = keep.tile([P, S], U32, name=name, align_bytes=64)
+            nc.vector.tensor_copy(picked[:], x_word_table[:].bitcast(U32).indirect(list_t[:]))
+            return picked
+
+        def round_weight(grouped, raw, first, count):
+            h, m0 = divmod(first, HALF // PACK)
+            dst = grouped[:].rearrange("p (t m j) -> p m j t", t=PACK, j=PACK)[:, first : first + count]
+            src = raw[h][:].rearrange("p j (m t) -> p m j t", t=PACK)[:, m0 : m0 + count]
+            nc.scalar.copy(out=dst, in_=src)
+
+        def mx_tiles(width, name):
+            codes = keep.tile([P, width], U32, name=name + "_codes", align_bytes=64)
+            scales = keep.tile([P, width], U8, name=name + "_scales", align_bytes=64)
+            return codes, scales
+
+        def quantize_into(operand, grouped, first, count):
+            nc.vector.quantize_mx(
+                out=operand[0][:, first : first + count].bitcast(FP8X4),
+                scales=operand[1][:, first : first + count],
+                in_=grouped[:, PACK * first : PACK * (first + count)],
+            )
+
+        def quantize(grouped, name):
+            width = grouped.shape[1] // PACK
+            operand = mx_tiles(width, name)
+            quantize_into(operand, grouped, 0, width)
+            return operand
+
+        def product(bank, lhs, cols, rhs):
+            acc = psum.tile([P, S], F32, name="acc", tag="bank%d" % bank)
+            nc.tensor.matmul_mx(
+                out=acc[:],
+                lhsT=lhs[0][:, cols].bitcast(FP8X4),
+                lhsT_scale=lhs[1][:, cols],
+                rhs=rhs[0][:].bitcast(FP8X4),
+                rhs_scale=rhs[1][:],
+                start=True,
+                stop=True,
+            )
+            return acc
+
+        xa_scales = gather_scales(offs_t, "xa_scales")
+        xb_scales = gather_scales(two_t, "xb_scales")
+
+        w1_grouped = keep.tile([P, PACK * H], BF16, name="w1_grouped", align_bytes=64)
+        for h in range(2):
+            round_weight(w1_grouped, w1_raw, 64 * h, 64)
+        w1_q = quantize(w1_grouped[:], "w1")
+        w2_raw = [load_weight_half(w2, "w2", h) for h in range(2)]
+
+        xa_words = gather_words(offs_t, "xa_words")
+        xb_words = gather_words(two_t, "xb_words")
+
+        half_sign = keep.tile([P, PACK], F32, name="half_sign")
+        gb_signed = keep.tile([P, PACK], F32, name="gb_signed")
+        nc.vector.tensor_scalar(half_sign[:], ga_t[:], 0.0, 0.5, ALU.is_ge, ALU.subtract)
+        nc.vector.scalar_tensor_tensor(gb_signed[:], half_sign[:], 2.0, gb_t[:], ALU.mult, ALU.mult)
+
+        w2_grouped = keep.tile([P, PACK * H], BF16, name="w2_grouped", tag="rounded", align_bytes=64)
+
+        def project_a(t, tag):
+            acc = product(t, w1_q, slice(P * t, P * (t + 1)), (xa_words, xa_scales))
+            a_t = keep.tile([P, S], F32, name="a_rows%d" % t, tag=tag)
+            nc.scalar.activation(out=a_t[:], in_=acc[:], func=ACT.Copy, scale=ga_abs[:, t : t + 1])
+            return a_t
+
+        def fetch(t):
+            fetched = keep.tile([P, S], F32, name="fetched%d" % t)
+            for h in range(2):
+                nc.vector.tensor_copy(
+                    fetched[:, h * HALF : (h + 1) * HALF], a_rows[t][:].indirect(n1_t[:, 16 * h : 16 * (h + 1)])
+                )
+            return fetched
+
+        a_rows = [project_a(0, "a0"), project_a(1, "a1")]
+        fetched = [fetch(0), fetch(1)]
+        for quarter in range(4):
+            round_weight(w2_grouped, w2_raw, 32 * quarter, 32)
+        w2_q = quantize(w2_grouped[:], "w2")
+        a_rows.extend([project_a(2, "stage1"), project_a(3, "stage0")])
+
+        z_rows = keep.tile([P, PACK, S], BF16, name="z_rows", tag="rounded", align_bytes=64)
+
+        def larger(t):
+            nc.vector.tensor_tensor(z_rows[:, t, :], fetched[t][:], a_rows[t][:], ALU.max)
+
+        larger(0)
+        larger(1)
+        z2_rows = keep.tile([P, PACK, V], BF16, name="z2_rows", tag="z2_rows", align_bytes=64)
+        for t in range(PACK):
+            acc = product(PACK + t, w2_q, slice(P * t, P * (t + 1)), (xb_words, xb_scales))
+            nc.scalar.activation(out=z2_rows[:, t, :], in_=acc[:], func=ACT.Copy, scale=gb_signed[:, t : t + 1])
+        fetched.extend([fetch(2), fetch(3)])
+        larger(2)
+        larger(3)
+
+        z2_grouped = keep.tile([P, PACK * V], BF16, name="z2_grouped", tag="z2_grouped", align_bytes=64)
+        dst = z2_grouped[:].rearrange("p (c i t) -> p c t i", i=4, t=PACK)
+        src = z2_rows[:].rearrange("p t (c i) -> p c t i", i=4)
+        z2_q = mx_tiles(V, "z2")
+        for h in range(2):
+            nc.scalar.copy(out=dst[:, 64 * h : 64 * (h + 1)], in_=src[:, 64 * h : 64 * (h + 1)])
+
+        def group_z(r, tag):
+            grouped = keep.tile([P, PACK * P], BF16, name="z_grouped%d" % r, tag=tag, align_bytes=64)
+            nc.vector.tensor_copy(
+                out=grouped[:].rearrange("p (c i t) -> p c t i", i=2, t=PACK),
+                in_=z_rows[:].rearrange("p t (c i r) -> p r c t i", i=2, r=PACK)[:, r],
+            )
+            return grouped
+
+        def scores(r, z_q):
+            acc = product(r, z_q, slice(0, P), z2_q)
+            s_r = keep.tile([P, V], F32, name="s_rows%d" % r)
+            nc.scalar.activation(out=s_r[:], in_=acc[:], func=ACT.Copy, scale=0.0625)
+            return s_r
+
+        z_grouped = [group_z(0, "zg0")]
+        quantize_into(z2_q, z2_grouped, 0, HALF)
+        z_q = [quantize(z_grouped[0][:], "z_tile0")]
+        z_grouped.append(group_z(1, "zg1"))
+        quantize_into(z2_q, z2_grouped, HALF, HALF)
+        s_rows = [scores(0, z_q[0])]
+        z_q.append(quantize(z_grouped[1][:], "z_tile1"))
+        s_rows.append(scores(1, z_q[1]))
+        z_grouped.extend([group_z(2, "z2_rows"), group_z(3, "z2_grouped")])
+        for r in (2, 3):
+            s_rows.append(scores(r, quantize(z_grouped[r][:], "z_tile%d" % r)))
+
+        out_rows = out.rearrange("(p r) v -> p r v", r=PACK)
+        parts = []
+        for r in range(PACK):
+            qv = keep.tile([P, W], F32, name="qv%d" % r)
+            diff = keep.tile([P, W], F32, name="diff%d" % r)
+            half_qv = keep.tile([P, W], F32, name="half_qv%d" % r)
+            lead = keep.tile([P, W], F32, name="lead%d" % r)
+            nc.vector.tensor_copy(qv[:], s_rows[r][:].indirect(lb_t[:]))
+            nc.vector.tensor_tensor(diff[:], s_rows[r][:].indirect(la_t[:]), qv[:], ALU.subtract)
+            nc.scalar.activation(out=half_qv[:], in_=qv[:], func=ACT.Copy, scale=0.5)
+            nc.scalar.activation(out=lead[:], in_=diff[:], func=ACT.Relu)
+            parts.append((qv, diff, half_qv, lead))
+        for pair in range(2):
+            placed = [keep.tile([P, V], F32, name="placed%d" % r) for r in (2 * pair, 2 * pair + 1)]
+            for i in range(2):
+                qv, diff, half_qv, lead = parts[2 * pair + i]
+                nc.vector.tensor_tensor(placed[i][:].indirect(la_t[:]), diff[:], half_qv[:], ALU.add)
+            for i in range(2):
+                qv, diff, half_qv, lead = parts[2 * pair + i]
+                nc.vector.tensor_tensor(placed[i][:].indirect(lb_t[:]), qv[:], lead[:], ALU.add)
+                nc.sync.dma_start(out=out_rows[:, 2 * pair + i, :], in_=placed[i][:])

@@ -37,7 +37,7 @@ def tile_picked_keyduel_none_p_kernel(tc, x_words, x_scales, w1, w2, ga, gb, off
         x_word_table = keep.tile([P, T], I32, name="x_word_table", align_bytes=64)
         nc.vector.memset(x_scale_table[:].bitcast(I32), 0)
         for q in range(4):
-            nc.scalar.dma_start(
+            nc.sync.dma_start(
                 out=x_scale_table[32 * q : 32 * q + 4, :].bitcast(I32),
                 in_=x_scales[0, 4 * q : 4 * q + 4, :].bitcast(I32),
             )
@@ -47,15 +47,13 @@ def tile_picked_keyduel_none_p_kernel(tc, x_words, x_scales, w1, w2, ga, gb, off
             nc.sync.dma_start(out=raw[:], in_=w.rearrange("(p j) c -> p j c", j=PACK)[:, :, h * HALF : (h + 1) * HALF])
             return raw
 
-        nc.sync.dma_start(offs_t[:], offs)
-        nc.sync.dma_start(two_t[:], two)
-        w1_raw = [load_weight_half(w1, "w1", h) for h in range(2)]
         ga_t = keep.tile([P, PACK], F32, name="ga_t")
-        gb_t = keep.tile([P, PACK], F32, name="gb_t")
-        nc.sync.dma_start(out=ga_t[:], in_=ga.rearrange("(p t) o -> p (t o)", t=PACK))
+        nc.scalar.dma_start(out=ga_t[:], in_=ga.rearrange("(p t) o -> p (t o)", t=PACK))
+        nc.sync.dma_start(offs_t[:], offs)
+        w1_raw = [load_weight_half(w1, "w1", h) for h in range(2)]
+        nc.sync.dma_start(two_t[:], two)
         nc.sync.dma_start(out=x_word_table[:], in_=x_words[0].rearrange("p n r -> p (n r)").bitcast(I32))
         nc.sync.dma_start(n1_t[:], n1)
-        nc.sync.dma_start(out=gb_t[:], in_=gb.rearrange("(p t) o -> p (t o)", t=PACK))
         nc.sync.dma_start(la_t[:], la)
         nc.sync.dma_start(lb_t[:], lb)
 
@@ -96,14 +94,14 @@ def tile_picked_keyduel_none_p_kernel(tc, x_words, x_scales, w1, w2, ga, gb, off
             quantize_into(operand, grouped, 0, width)
             return operand
 
-        def product(bank, lhs, cols, rhs):
-            acc = psum.tile([P, S], F32, name="acc", tag="bank%d" % bank)
+        def product(bank, lhs, cols, rhs, moving=slice(0, S)):
+            acc = psum.tile([P, moving.stop - moving.start], F32, name="acc", tag="bank%d" % bank)
             nc.tensor.matmul_mx(
                 out=acc[:],
                 lhsT=lhs[0][:, cols].bitcast(FP8X4),
                 lhsT_scale=lhs[1][:, cols],
-                rhs=rhs[0][:].bitcast(FP8X4),
-                rhs_scale=rhs[1][:],
+                rhs=rhs[0][:, moving].bitcast(FP8X4),
+                rhs_scale=rhs[1][:, moving],
                 start=True,
                 stop=True,
             )
@@ -112,17 +110,24 @@ def tile_picked_keyduel_none_p_kernel(tc, x_words, x_scales, w1, w2, ga, gb, off
         xa_scales = gather_scales(offs_t, "xa_scales")
         xb_scales = gather_scales(two_t, "xb_scales")
 
-        w1_grouped = keep.tile([P, PACK * H], BF16, name="w1_grouped", align_bytes=64)
+        w1_grouped = keep.tile([P, PACK * H], BF16, name="w1_grouped", tag="w1_grouped", align_bytes=64)
         for h in range(2):
             round_weight(w1_grouped, w1_raw, 64 * h, 64)
         w1_q = quantize(w1_grouped[:], "w1")
         w2_raw = [load_weight_half(w2, "w2", h) for h in range(2)]
+        gb_t = keep.tile([P, PACK], F32, name="gb_t", tag="w1_grouped", align_bytes=64)
+        nc.sync.dma_start(out=gb_t[:], in_=gb.rearrange("(p t) o -> p (t o)", t=PACK))
 
-        xa_words = gather_words(offs_t, "xa_words")
+        xa_words = keep.tile([P, S], U32, name="xa_words", align_bytes=64)
+        for h in range(2):
+            nc.vector.tensor_copy(
+                xa_words[:, h * HALF : (h + 1) * HALF],
+                x_word_table[:].bitcast(U32).indirect(offs_t[:, 16 * h : 16 * (h + 1)]),
+            )
         xb_words = gather_words(two_t, "xb_words")
 
         half_sign = keep.tile([P, PACK], F32, name="half_sign")
-        gb_signed = keep.tile([P, PACK], F32, name="gb_signed")
+        gb_signed = keep.tile([P, PACK], F32, name="gb_signed", tag="zg0", align_bytes=64)
         nc.vector.tensor_scalar(half_sign[:], ga_t[:], 0.0, 0.5, ALU.is_ge, ALU.subtract)
         nc.vector.scalar_tensor_tensor(gb_signed[:], half_sign[:], 2.0, gb_t[:], ALU.mult, ALU.mult)
 
@@ -142,7 +147,12 @@ def tile_picked_keyduel_none_p_kernel(tc, x_words, x_scales, w1, w2, ga, gb, off
                 )
             return fetched
 
-        a_rows = [project_a(0, "a0"), project_a(1, "a1")]
+        a_first = keep.tile([P, S], F32, name="a_rows0")
+        for h in range(2):
+            cols = slice(h * HALF, (h + 1) * HALF)
+            acc = product(PACK * h, w1_q, slice(0, P), (xa_words, xa_scales), cols)
+            nc.scalar.activation(out=a_first[:, cols], in_=acc[:], func=ACT.Copy, scale=ga_abs[:, 0:1])
+        a_rows = [a_first, project_a(1, "a1")]
         fetched = [fetch(0), fetch(1)]
         for quarter in range(4):
             round_weight(w2_grouped, w2_raw, 32 * quarter, 32)
@@ -167,13 +177,11 @@ def tile_picked_keyduel_none_p_kernel(tc, x_words, x_scales, w1, w2, ga, gb, off
         z2_grouped = keep.tile([P, PACK * V], BF16, name="z2_grouped", tag="z2_grouped", align_bytes=64)
         dst = z2_grouped[:].rearrange("p (c i t) -> p c t i", i=4, t=PACK)
         src = z2_rows[:].rearrange("p t (c i) -> p c t i", i=4)
-        z2_q = mx_tiles(V, "z2")
-        for h in range(2):
-            nc.scalar.copy(out=dst[:, 64 * h : 64 * (h + 1)], in_=src[:, 64 * h : 64 * (h + 1)])
+        nc.scalar.copy(out=dst[:, 0:64], in_=src[:, 0:64])
 
-        def group_z(r, tag):
+        def group_z(r, tag, copy=nc.vector.tensor_copy):
             grouped = keep.tile([P, PACK * P], BF16, name="z_grouped%d" % r, tag=tag, align_bytes=64)
-            nc.vector.tensor_copy(
+            copy(
                 out=grouped[:].rearrange("p (c i t) -> p c t i", i=2, t=PACK),
                 in_=z_rows[:].rearrange("p t (c i r) -> p r c t i", i=2, r=PACK)[:, r],
             )
@@ -185,36 +193,42 @@ def tile_picked_keyduel_none_p_kernel(tc, x_words, x_scales, w1, w2, ga, gb, off
             nc.scalar.activation(out=s_r[:], in_=acc[:], func=ACT.Copy, scale=0.0625)
             return s_r
 
+        nc.vector.tensor_copy(out=dst[:, 64:96], in_=src[:, 64:96])
         z_grouped = [group_z(0, "zg0")]
-        quantize_into(z2_q, z2_grouped, 0, HALF)
+        nc.vector.tensor_copy(out=dst[:, 96:128], in_=src[:, 96:128])
         z_q = [quantize(z_grouped[0][:], "z_tile0")]
-        z_grouped.append(group_z(1, "zg1"))
-        quantize_into(z2_q, z2_grouped, HALF, HALF)
-        s_rows = [scores(0, z_q[0])]
-        z_q.append(quantize(z_grouped[1][:], "z_tile1"))
-        s_rows.append(scores(1, z_q[1]))
-        z_grouped.extend([group_z(2, "z2_rows"), group_z(3, "z2_grouped")])
+        z_last = group_z(3, "zg3", nc.scalar.copy)
+        z2_q = mx_tiles(V, "z2")
+        s_first = keep.tile([P, V], F32, name="s_rows0")
+        for h in range(2):
+            cols = slice(h * HALF, (h + 1) * HALF)
+            quantize_into(z2_q, z2_grouped, h * HALF, HALF)
+            acc = product(PACK * h, z_q[0], slice(0, P), z2_q, cols)
+            nc.scalar.activation(out=s_first[:, cols], in_=acc[:], func=ACT.Copy, scale=0.0625)
+        s_rows = [s_first]
+        z_grouped.extend([group_z(1, "z2_rows"), group_z(2, "z2_grouped"), z_last])
+        s_rows.append(scores(1, quantize(z_grouped[1][:], "z_tile1")))
         for r in (2, 3):
             s_rows.append(scores(r, quantize(z_grouped[r][:], "z_tile%d" % r)))
 
         out_rows = out.rearrange("(p r) v -> p r v", r=PACK)
-        parts = []
+        half_qv, qv, diff, lead = [], [], [], []
         for r in range(PACK):
-            qv = keep.tile([P, W], F32, name="qv%d" % r)
-            diff = keep.tile([P, W], F32, name="diff%d" % r)
-            half_qv = keep.tile([P, W], F32, name="half_qv%d" % r)
-            lead = keep.tile([P, W], F32, name="lead%d" % r)
-            nc.vector.tensor_copy(qv[:], s_rows[r][:].indirect(lb_t[:]))
-            nc.vector.tensor_tensor(diff[:], s_rows[r][:].indirect(la_t[:]), qv[:], ALU.subtract)
-            nc.scalar.activation(out=half_qv[:], in_=qv[:], func=ACT.Copy, scale=0.5)
-            nc.scalar.activation(out=lead[:], in_=diff[:], func=ACT.Relu)
-            parts.append((qv, diff, half_qv, lead))
-        for pair in range(2):
-            placed = [keep.tile([P, V], F32, name="placed%d" % r) for r in (2 * pair, 2 * pair + 1)]
-            for i in range(2):
-                qv, diff, half_qv, lead = parts[2 * pair + i]
-                nc.vector.tensor_tensor(placed[i][:].indirect(la_t[:]), diff[:], half_qv[:], ALU.add)
-            for i in range(2):
-                qv, diff, half_qv, lead = parts[2 * pair + i]
-                nc.vector.tensor_tensor(placed[i][:].indirect(lb_t[:]), qv[:], lead[:], ALU.add)
-                nc.sync.dma_start(out=out_rows[:, 2 * pair + i, :], in_=placed[i][:])
+            half_qv.append(keep.tile([P, W], F32, name="half_qv%d" % r))
+            nc.vector.tensor_scalar(half_qv[r][:], s_rows[r][:].indirect(lb_t[:]), 0.5, 0.0, ALU.mult, ALU.add)
+        for r in range(PACK):
+            qv.append(keep.tile([P, W], F32, name="qv%d" % r))
+            nc.scalar.activation(out=qv[r][:], in_=half_qv[r][:], func=ACT.Copy, scale=2.0)
+        for r in range(PACK):
+            diff.append(keep.tile([P, W], F32, name="diff%d" % r))
+            nc.vector.tensor_tensor(diff[r][:], s_rows[r][:].indirect(la_t[:]), qv[r][:], ALU.subtract)
+        for r in range(PACK):
+            lead.append(keep.tile([P, W], F32, name="lead%d" % r))
+            nc.scalar.activation(out=lead[r][:], in_=diff[r][:], func=ACT.Relu)
+        for pair in ((0, 1), (2, 3)):
+            placed = {r: keep.tile([P, V], F32, name="placed%d" % r) for r in pair}
+            for r in pair:
+                nc.vector.tensor_tensor(placed[r][:].indirect(la_t[:]), diff[r][:], half_qv[r][:], ALU.add)
+            for r in pair:
+                nc.vector.tensor_tensor(placed[r][:].indirect(lb_t[:]), qv[r][:], lead[r][:], ALU.add)
+                nc.sync.dma_start(out=out_rows[:, r, :], in_=placed[r][:])

@@ -131,7 +131,7 @@ def tile_picked_keyduel_none_p_kernel(tc, x_words, x_scales, w1, w2, ga, gb, off
         nc.vector.tensor_scalar(half_sign[:], ga_t[:], 0.0, 0.5, ALU.is_ge, ALU.subtract)
         nc.vector.scalar_tensor_tensor(gb_signed[:], half_sign[:], 2.0, gb_t[:], ALU.mult, ALU.mult)
 
-        w2_grouped = keep.tile([P, PACK * H], BF16, name="w2_grouped", tag="rounded", align_bytes=64)
+        w2_grouped = keep.tile([P, PACK * H], BF16, name="w2_grouped", align_bytes=64)
 
         def project_a(t, tag):
             acc = product(t, w1_q, slice(P * t, P * (t + 1)), (xa_words, xa_scales))
@@ -139,13 +139,15 @@ def tile_picked_keyduel_none_p_kernel(tc, x_words, x_scales, w1, w2, ga, gb, off
             nc.scalar.activation(out=a_t[:], in_=acc[:], func=ACT.Copy, scale=ga_abs[:, t : t + 1])
             return a_t
 
+        fetched = keep.tile([P, PACK, S], BF16, name="fetched")
+        in_place = keep.tile([P, PACK, S], BF16, name="in_place")
+
         def fetch(t):
-            fetched = keep.tile([P, S], F32, name="fetched%d" % t)
+            nc.gpsimd.tensor_scalar(in_place[:, t, :], a_rows[t][:], 1.0, 0.0, ALU.mult, ALU.add)
             for h in range(2):
                 nc.vector.tensor_copy(
-                    fetched[:, h * HALF : (h + 1) * HALF], a_rows[t][:].indirect(n1_t[:, 16 * h : 16 * (h + 1)])
+                    fetched[:, t, h * HALF : (h + 1) * HALF], a_rows[t][:].indirect(n1_t[:, 16 * h : 16 * (h + 1)])
                 )
-            return fetched
 
         a_first = keep.tile([P, S], F32, name="a_rows0")
         for h in range(2):
@@ -153,24 +155,29 @@ def tile_picked_keyduel_none_p_kernel(tc, x_words, x_scales, w1, w2, ga, gb, off
             acc = product(PACK * h, w1_q, slice(0, P), (xa_words, xa_scales), cols)
             nc.scalar.activation(out=a_first[:, cols], in_=acc[:], func=ACT.Copy, scale=ga_abs[:, 0:1])
         a_rows = [a_first, project_a(1, "a1")]
-        fetched = [fetch(0), fetch(1)]
-        for quarter in range(4):
-            round_weight(w2_grouped, w2_raw, 32 * quarter, 32)
-        w2_q = quantize(w2_grouped[:], "w2")
-        a_rows.extend([project_a(2, "stage1"), project_a(3, "stage0")])
-
-        z_rows = keep.tile([P, PACK, S], BF16, name="z_rows", tag="rounded", align_bytes=64)
+        z_rows = keep.tile([P, PACK, S], BF16, name="z_rows")
 
         def larger(t):
-            nc.vector.tensor_tensor(z_rows[:, t, :], fetched[t][:], a_rows[t][:], ALU.max)
+            nc.vector.tensor_tensor(z_rows[:, t, :], fetched[:, t, :], in_place[:, t, :], ALU.max)
 
+        fetch(0)
+        fetch(1)
         larger(0)
         larger(1)
+        for quarter in range(4):
+            round_weight(w2_grouped, w2_raw, 32 * quarter, 32)
+        w2_q = mx_tiles(H, "w2")
+        for h in range(2):
+            quantize_into(w2_q, w2_grouped, h * HALF, HALF)
+        a_rows.extend([project_a(2, "stage1"), project_a(3, "stage0")])
+
+
         z2_rows = keep.tile([P, PACK, V], BF16, name="z2_rows", tag="z2_rows", align_bytes=64)
         for t in range(PACK):
             acc = product(PACK + t, w2_q, slice(P * t, P * (t + 1)), (xb_words, xb_scales))
             nc.scalar.activation(out=z2_rows[:, t, :], in_=acc[:], func=ACT.Copy, scale=gb_signed[:, t : t + 1])
-        fetched.extend([fetch(2), fetch(3)])
+        fetch(2)
+        fetch(3)
         larger(2)
         larger(3)
 
@@ -197,7 +204,7 @@ def tile_picked_keyduel_none_p_kernel(tc, x_words, x_scales, w1, w2, ga, gb, off
         z_grouped = [group_z(0, "zg0")]
         nc.vector.tensor_copy(out=dst[:, 96:128], in_=src[:, 96:128])
         z_q = [quantize(z_grouped[0][:], "z_tile0")]
-        z_last = group_z(3, "zg3", nc.scalar.copy)
+        z_late = [group_z(r, "zg%d" % r, nc.scalar.copy) for r in (2, 3)]
         z2_q = mx_tiles(V, "z2")
         s_first = keep.tile([P, V], F32, name="s_rows0")
         for h in range(2):
@@ -206,7 +213,7 @@ def tile_picked_keyduel_none_p_kernel(tc, x_words, x_scales, w1, w2, ga, gb, off
             acc = product(PACK * h, z_q[0], slice(0, P), z2_q, cols)
             nc.scalar.activation(out=s_first[:, cols], in_=acc[:], func=ACT.Copy, scale=0.0625)
         s_rows = [s_first]
-        z_grouped.extend([group_z(1, "z2_rows"), group_z(2, "z2_grouped"), z_last])
+        z_grouped.extend([group_z(1, "z2_grouped")] + z_late)
         s_rows.append(scores(1, quantize(z_grouped[1][:], "z_tile1")))
         for r in (2, 3):
             s_rows.append(scores(r, quantize(z_grouped[r][:], "z_tile%d" % r)))

from contextlib import ExitStack

import concourse.mybir as mybir

K, T, S, V, H, W = 512, 2048, 512, 512, 512, 256
FLOPS = 2 * K * H * S + 2 * K * H * V + 2 * H * S * V

F32 = mybir.dt.float32
BF16 = mybir.dt.bfloat16
I32 = mybir.dt.int32
U32 = mybir.dt.uint32
U16 = mybir.dt.uint16
U8 = mybir.dt.uint8
FP8X4 = mybir.dt.float8_e4m3fn_x4
ALU = mybir.AluOpType
ACT = mybir.ActivationFunctionType

P = 128
PACK = 4
HALF = 256


def tile_picked_keyduel_none_p_kernel(tc, x_words, x_scales, w1, w2, ga, gb, offs, two, n1, la, lb, out):
    nc = tc.nc
    with ExitStack() as ctx:
        lists = ctx.enter_context(tc.tile_pool(name="lists", bufs=1))
        keep = ctx.enter_context(tc.tile_pool(name="keep", bufs=1))
        psum = ctx.enter_context(tc.psum_pool(name="psum", bufs=1))

        offs_t = lists.tile([P, S // 16], U16, name="offs_t")
        two_t = lists.tile([P, V // 16], U16, name="two_t")
        n1_t = lists.tile([P, S // 16], U16, name="n1_t")
        la_t = lists.tile([P, W // 16], U16, name="la_t")
        lb_t = lists.tile([P, W // 16], U16, name="lb_t")

        x_scale_table = keep.tile([P, T], U8, name="x_scale_table", align_bytes=64)
        x_word_table = keep.tile([P, T], I32, name="x_word_table", align_bytes=64)
        nc.vector.memset(x_scale_table[:].bitcast(I32), 0)
        for q in range(4):
            nc.sync.dma_start(
                out=x_scale_table[32 * q : 32 * q + 4, :].bitcast(I32),
                in_=x_scales[0, 4 * q : 4 * q + 4, :].bitcast(I32),
            )

        def load_weight_half(w, name, h):
            raw = keep.tile([P, PACK, HALF], F32, name="%s_raw%d" % (name, h), tag="stage%d" % h)
            nc.sync.dma_start(out=raw[:], in_=w.rearrange("(p j) c -> p j c", j=PACK)[:, :, h * HALF : (h + 1) * HALF])
            return raw

        ga_t = keep.tile([P, PACK], F32, name="ga_t")
        nc.scalar.dma_start(out=ga_t[:], in_=ga.rearrange("(p t) o -> p (t o)", t=PACK))
        nc.sync.dma_start(offs_t[:], offs)
        w1_raw = [load_weight_half(w1, "w1", h) for h in range(2)]
        nc.sync.dma_start(two_t[:], two)
        nc.sync.dma_start(out=x_word_table[:], in_=x_words[0].rearrange("p n r -> p (n r)").bitcast(I32))
        nc.sync.dma_start(n1_t[:], n1)
        nc.sync.dma_start(la_t[:], la)
        nc.sync.dma_start(lb_t[:], lb)

        ga_abs = keep.tile([P, PACK], F32, name="ga_abs")
        nc.scalar.activation(out=ga_abs[:], in_=ga_t[:], func=ACT.Abs)

        def gather_scales(list_t, name):
            picked = keep.tile([P, S], U8, name=name, align_bytes=64)
            nc.vector.tensor_copy(picked[:], x_scale_table[:].indirect(list_t[:]))
            return picked

        def gather_words(list_t, name):
            picked = keep.tile([P, S], U32, name=name, align_bytes=64)
            nc.vector.tensor_copy(picked[:], x_word_table[:].bitcast(U32).indirect(list_t[:]))
            return picked

        def round_weight(grouped, raw, first, count):
            h, m0 = divmod(first, HALF // PACK)
            dst = grouped[:].rearrange("p (t m j) -> p m j t", t=PACK, j=PACK)[:, first : first + count]
            src = raw[h][:].rearrange("p j (m t) -> p m j t", t=PACK)[:, m0 : m0 + count]
            nc.scalar.copy(out=dst, in_=src)

        def mx_tiles(width, name):
            codes = keep.tile([P, width], U32, name=name + "_codes", align_bytes=64)
            scales = keep.tile([P, width], U8, name=name + "_scales", align_bytes=64)
            return codes, scales

        def quantize_into(operand, grouped, first, count):
            nc.vector.quantize_mx(
                out=operand[0][:, first : first + count].bitcast(FP8X4),
                scales=operand[1][:, first : first + count],
                in_=grouped[:, PACK * first : PACK * (first + count)],
            )

        def quantize(grouped, name):
            width = grouped.shape[1] // PACK
            operand = mx_tiles(width, name)
            quantize_into(operand, grouped, 0, width)
            return operand

        def product(bank, lhs, cols, rhs, moving=slice(0, S)):
            acc = psum.tile([P, moving.stop - moving.start], F32, name="acc", tag="bank%d" % bank)
            nc.tensor.matmul_mx(
                out=acc[:],
                lhsT=lhs[0][:, cols].bitcast(FP8X4),
                lhsT_scale=lhs[1][:, cols],
                rhs=rhs[0][:, moving].bitcast(FP8X4),
                rhs_scale=rhs[1][:, moving],
                start=True,
                stop=True,
            )
            return acc

        xa_scales = gather_scales(offs_t, "xa_scales")
        xb_scales = gather_scales(two_t, "xb_scales")

        w1_grouped = keep.tile([P, PACK * H], BF16, name="w1_grouped", tag="w1_grouped", align_bytes=64)
        for h in range(2):
            round_weight(w1_grouped, w1_raw, 64 * h, 64)
        w1_q = quantize(w1_grouped[:], "w1")
        w2_raw = [load_weight_half(w2, "w2", h) for h in range(2)]
        gb_t = keep.tile([P, PACK], F32, name="gb_t", tag="w1_grouped", align_bytes=64)
        nc.sync.dma_start(out=gb_t[:], in_=gb.rearrange("(p t) o -> p (t o)", t=PACK))

        xa_words = keep.tile([P, S], U32, name="xa_words", align_bytes=64)
        for h in range(2):
            nc.vector.tensor_copy(
                xa_words[:, h * HALF : (h + 1) * HALF],
                x_word_table[:].bitcast(U32).indirect(offs_t[:, 16 * h : 16 * (h + 1)]),
            )
        xb_words = gather_words(two_t, "xb_words")

        half_sign = keep.tile([P, PACK], F32, name="half_sign")
        gb_signed = keep.tile([P, PACK], F32, name="gb_signed", tag="zg0", align_bytes=64)
        nc.vector.tensor_scalar(half_sign[:], ga_t[:], 0.0, 0.5, ALU.is_ge, ALU.subtract)
        nc.vector.scalar_tensor_tensor(gb_signed[:], half_sign[:], 2.0, gb_t[:], ALU.mult, ALU.mult)

        w2_grouped = keep.tile([P, PACK * H], BF16, name="w2_grouped", align_bytes=64)

        def project_a(t, tag):
            acc = product(t, w1_q, slice(P * t, P * (t + 1)), (xa_words, xa_scales))
            a_t = keep.tile([P, S], F32, name="a_rows%d" % t, tag=tag)
            nc.scalar.activation(out=a_t[:], in_=acc[:], func=ACT.Copy, scale=ga_abs[:, t : t + 1])
            return a_t

        fetched = keep.tile([P, PACK, S], BF16, name="fetched")
        in_place = keep.tile([P, PACK, S], BF16, name="in_place")

        def fetch(t):
            nc.gpsimd.tensor_scalar(in_place[:, t, :], a_rows[t][:], 1.0, 0.0, ALU.mult, ALU.add)
            for h in range(2):
                nc.vector.tensor_copy(
                    fetched[:, t, h * HALF : (h + 1) * HALF], a_rows[t][:].indirect(n1_t[:, 16 * h : 16 * (h + 1)])
                )

        a_first = keep.tile([P, S], F32, name="a_rows0")
        for h in range(2):
            cols = slice(h * HALF, (h + 1) * HALF)
            acc = product(PACK * h, w1_q, slice(0, P), (xa_words, xa_scales), cols)
            nc.scalar.activation(out=a_first[:, cols], in_=acc[:], func=ACT.Copy, scale=ga_abs[:, 0:1])
        a_rows = [a_first, project_a(1, "a1")]
        z_rows = keep.tile([P, PACK, S], BF16, name="z_rows")

        def larger(t):
            nc.vector.tensor_tensor(z_rows[:, t, :], fetched[:, t, :], in_place[:, t, :], ALU.max)

        fetch(0)
        fetch(1)
        larger(0)
        larger(1)
        for quarter in range(4):
            round_weight(w2_grouped, w2_raw, 32 * quarter, 32)
        w2_q = mx_tiles(H, "w2")
        for h in range(2):
            quantize_into(w2_q, w2_grouped, h * HALF, HALF)
        a_rows.extend([project_a(2, "stage1"), project_a(3, "stage0")])


        z2_rows = keep.tile([P, PACK, V], BF16, name="z2_rows", tag="z2_rows", align_bytes=64)
        for t in range(PACK):
            acc = product(PACK + t, w2_q, slice(P * t, P * (t + 1)), (xb_words, xb_scales))
            nc.scalar.activation(out=z2_rows[:, t, :], in_=acc[:], func=ACT.Copy, scale=gb_signed[:, t : t + 1])
        fetch(2)
        fetch(3)
        larger(2)
        larger(3)

        z2_grouped = keep.tile([P, PACK * V], BF16, name="z2_grouped", tag="z2_grouped", align_bytes=64)
        dst = z2_grouped[:].rearrange("p (c i t) -> p c t i", i=4, t=PACK)
        src = z2_rows[:].rearrange("p t (c i) -> p c t i", i=4)
        nc.scalar.copy(out=dst[:, 0:64], in_=src[:, 0:64])

        def group_z(r, tag, copy=nc.vector.tensor_copy):
            grouped = keep.tile([P, PACK * P], BF16, name="z_grouped%d" % r, tag=tag, align_bytes=64)
            copy(
                out=grouped[:].rearrange("p (c i t) -> p c t i", i=2, t=PACK),
                in_=z_rows[:].rearrange("p t (c i r) -> p r c t i", i=2, r=PACK)[:, r],
            )
            return grouped

        def scores(r, z_q):
            acc = product(r, z_q, slice(0, P), z2_q)
            s_r = keep.tile([P, V], F32, name="s_rows%d" % r)
            nc.scalar.activation(out=s_r[:], in_=acc[:], func=ACT.Copy, scale=0.0625)
            return s_r

        nc.vector.tensor_copy(out=dst[:, 64:96], in_=src[:, 64:96])
        z_grouped = [group_z(0, "zg0")]
        nc.vector.tensor_copy(out=dst[:, 96:128], in_=src[:, 96:128])
        z_q = [quantize(z_grouped[0][:], "z_tile0")]
        z_late = [group_z(r, "zg%d" % r, nc.scalar.copy) for r in (2, 3)]
        z2_q = mx_tiles(V, "z2")
        s_first = keep.tile([P, V], F32, name="s_rows0")
        for h in range(2):
            cols = slice(h * HALF, (h + 1) * HALF)
            quantize_into(z2_q, z2_grouped, h * HALF, HALF)
            acc = product(PACK * h, z_q[0], slice(0, P), z2_q, cols)
            nc.scalar.activation(out=s_first[:, cols], in_=acc[:], func=ACT.Copy, scale=0.0625)
        s_rows = [s_first]
        z_grouped.extend([group_z(1, "z2_grouped")] + z_late)
        s_rows.append(scores(1, quantize(z_grouped[1][:], "z_tile1")))
        for r in (2, 3):
            s_rows.append(scores(r, quantize(z_grouped[r][:], "z_tile%d" % r)))

        out_rows = out.rearrange("(p r) v -> p r v", r=PACK)
        half_qv, qv, diff, lead = [], [], [], []
        for r in range(PACK):
            half_qv.append(keep.tile([P, W], F32, name="half_qv%d" % r))
            nc.vector.tensor_scalar(half_qv[r][:], s_rows[r][:].indirect(lb_t[:]), 0.5, 0.0, ALU.mult, ALU.add)
        for r in range(PACK):
            qv.append(keep.tile([P, W], F32, name="qv%d" % r))
            nc.scalar.activation(out=qv[r][:], in_=half_qv[r][:], func=ACT.Copy, scale=2.0)
        for r in range(PACK):
            diff.append(keep.tile([P, W], F32, name="diff%d" % r))
            nc.vector.tensor_tensor(diff[r][:], s_rows[r][:].indirect(la_t[:]), qv[r][:], ALU.subtract)
        for r in range(PACK):
            lead.append(keep.tile([P, W], F32, name="lead%d" % r))
            nc.scalar.activation(out=lead[r][:], in_=diff[r][:], func=ACT.Relu)
        for pair in ((0, 1), (2, 3)):
            placed = {r: keep.tile([P, V], F32, name="placed%d" % r) for r in pair}
            for r in pair:
                nc.vector.tensor_tensor(placed[r][:].indirect(la_t[:]), diff[r][:], half_qv[r][:], ALU.add)
            for r in pair:
                nc.vector.tensor_tensor(placed[r][:].indirect(lb_t[:]), qv[r][:], lead[r][:], ALU.add)
                nc.sync.dma_start(out=out_rows[:, r, :], in_=placed[r][:])
